import numpy as np
import ml_dtypes


def mxq(x, axis, fmt="e4m3"):
    dtype, down = {"e4m3": (ml_dtypes.float8_e4m3fn, 7), "e5m2": (ml_dtypes.float8_e5m2, 14)}[fmt]
    v = np.moveaxis(np.asarray(x, np.float32).astype(ml_dtypes.bfloat16).astype(np.float64), axis, -1)
    blocks = v.reshape(v.shape[:-1] + (-1, 32))
    amax = np.abs(blocks).max(-1, keepdims=True)
    byte = np.maximum(np.where(amax > 0, np.frexp(amax)[1] - 1 + 127, 0) - down, 1)
    scale = np.exp2(byte - 127.0)
    codes = (blocks / scale).astype(np.float32).astype(dtype).astype(np.float64)
    return np.moveaxis((codes * scale).reshape(v.shape), -1, axis)


WIDE = False


def mx_kscale(k):
    if not WIDE:
        return np.ones(k)
    levels = np.array([10, -10, 5, -5, 0])
    if k % 512:
        return np.exp2(np.random.permutation(np.resize(levels, k // 32))).repeat(32)
    a = np.empty((k // 512, 16))
    for p in range(k // 512):
        a[p, :8] = np.random.permutation(np.resize(levels, 8))
        for g in range(8):
            far = levels[np.abs(levels - a[p, g]) >= 10]
            a[p, g + 8] = far[np.random.randint(len(far))]
    return np.exp2(a.ravel()).repeat(32)


def f64(x):
    return np.asarray(x).astype(np.float64)


def striped(idx):
    return np.tile(idx.reshape(-1, 16).T, (8, 1)).astype(np.uint16)


def unstriped(offs):
    return offs[:16].T.reshape(-1).astype(np.int64)


def striped8(idx):
    return np.concatenate([x.reshape(-1, 16).T for x in idx]).astype(np.uint16)


def runs(offs, k):
    lists = np.stack([offs[16 * r : 16 * r + 16].T.reshape(-1) for r in range(8)]).astype(np.int64)
    return lists[np.arange(k) % 512 // 64]


def pack_weight(w):
    k, n = w.shape
    w = f64(np.asarray(w, np.float32).astype(ml_dtypes.bfloat16)).reshape(k // 32, 32, n)
    amax = np.abs(w).max(1)
    byte = np.clip(np.where(amax > 0, np.frexp(amax)[1] - 1 + 127 - 7, 1), 1, 254)
    scaled = (w * np.exp2(127.0 - byte)[:, None, :]).reshape(k, n).astype(np.float32)
    words = np.ascontiguousarray(scaled.reshape(k // 512, 128, 4, n).transpose(0, 1, 3, 2)).astype(ml_dtypes.float8_e4m3fn).view(np.uint8)
    return words, np.ascontiguousarray(byte.astype(np.uint8).reshape(k // 512, 16, n))


def unpack_weight(words, scales):
    g, p, n, _ = words.shape
    vals = np.ascontiguousarray(words).view(ml_dtypes.float8_e4m3fn).astype(np.float64) * np.repeat(np.exp2(scales.astype(np.float64) - 127.0), 8, axis=1)[..., None]
    return vals.transpose(0, 1, 3, 2).reshape(g * 512, n)


K, T, S, H, C = 512, 2048, 512, 512, 512


def setup_inputs():
    n = np.random.standard_normal
    s = mx_kscale(K)[:, None]
    packed_xT = pack_weight(n((K, T)) * s)
    return {
        "x_words": packed_xT[0],
        "x_scales": packed_xT[1],
        "w1": (n((K, H)) / np.sqrt(K) / s).astype(np.float32),
        "gs": (np.random.uniform(0.5, 1.5, (K, 1)) / s).astype(np.float32),
        "offs": striped(np.random.permutation(T)[:S]),
        "n1": striped8(np.stack([np.random.permutation(S) for _ in range(8)])),
        "n2": striped8(np.stack([np.random.permutation(S) for _ in range(8)])),
        "ca": striped(np.random.permutation(T)[:C]),
        "cb": striped(np.random.permutation(T)[:C]),
        "n3": striped8(np.stack([np.random.permutation(S) for _ in range(8)])),
        "n4": striped8(np.stack([np.random.permutation(S) for _ in range(8)])),
    }


def reference(x_words, x_scales, w1, gs, offs, n1, n2, ca, cb, n3, n4):
    x_ca = unpack_weight(x_words, x_scales)[:, unstriped(ca)]
    xq = unpack_weight(x_words, x_scales)[:, unstriped(offs)]
    y = mxq(f64(w1), 0, "e4m3").T @ xq
    z = f64(gs) * (y * (y[np.arange(H)[:, None], runs(n1, H)] - (y[np.arange(H)[:, None], runs(n2, H)])))
    zq = mxq(z, 0, "e4m3")
    a = 0.0625 * (x_ca.T @ zq)
    x_cb = unpack_weight(x_words, x_scales)[:, unstriped(cb)]
    b = 0.0625 * (x_cb.T @ zq)
    return (a - (a[np.arange(C)[:, None], runs(n3, C)])) / (np.abs(b) + np.abs(b[np.arange(C)[:, None], runs(n4, C)]) + 0.5)

@@ -1,0 +1,260 @@
+from contextlib import ExitStack
+
+import concourse.mybir as mybir
+
+K, T, S, H, C = 512, 2048, 512, 512, 512
+FLOPS = 2 * K * H * S + 2 * 2 * H * C * S
+
+F32 = mybir.dt.float32
+BF16 = mybir.dt.bfloat16
+I32 = mybir.dt.int32
+U32 = mybir.dt.uint32
+U16 = mybir.dt.uint16
+U8 = mybir.dt.uint8
+FP8X4 = mybir.dt.float8_e4m3fn_x4
+ALU = mybir.AluOpType
+ACT = mybir.ActivationFunctionType
+
+P = 128
+PACK = 4
+HALF = S // 2
+LIST_COLS = S // 16
+RUN = 8
+
+
+def tile_picked_ccmpnormbwind_none_p_kernel(
+    tc, x_words, x_scales, w1, gs, offs, n1, n2, ca, cb, n3, n4, out
+):
+    nc = tc.nc
+    with ExitStack() as ctx:
+        lists = ctx.enter_context(tc.tile_pool(name="lists", bufs=1))
+        sb = ctx.enter_context(tc.tile_pool(name="sb", bufs=1))
+        psum = ctx.enter_context(tc.psum_pool(name="psum", bufs=1))
+
+        def load_list(src, name):
+            dst = lists.tile([P, LIST_COLS], U16, name=name)
+            nc.sync.dma_start(dst[:], src)
+            return dst
+
+        def half_cols(h):
+            return slice(h * HALF, (h + 1) * HALF)
+
+        def half_list(lst, h):
+            return lst[:, h * (LIST_COLS // 2) : (h + 1) * (LIST_COLS // 2)]
+
+        scale_table = sb.tile([P, T], U8, name="scale_table", align_bytes=64)
+        nc.vector.memset(scale_table[:].bitcast(I32), 0)
+        half_const = sb.tile([P, 1], F32, name="half_const")
+        nc.vector.memset(half_const[:], 0.5)
+        warm = sb.tile([P, 1], F32, name="warm")
+        nc.scalar.activation(warm[:], half_const[:], ACT.Abs_reciprocal_sqrt)
+
+        for q in range(4):
+            nc.sync.dma_start(
+                scale_table[32 * q : 32 * q + 4, :].bitcast(I32),
+                x_scales[0, 4 * q : 4 * q + 4, :].bitcast(I32),
+            )
+        offs_l = load_list(offs, "offs_l")
+        cb_l = load_list(cb, "cb_l")
+        w_raw = []
+        for h in range(2):
+            w_half = sb.tile([P, PACK, H // 2], F32, name=f"w_raw{h}")
+            nc.sync.dma_start(
+                w_half[:], w1[:, h * (H // 2) : (h + 1) * (H // 2)].rearrange("(p j) c -> p j c", j=PACK)
+            )
+            w_raw.append(w_half)
+        word_table = sb.tile([P, T], U32, name="word_table", align_bytes=64)
+        nc.sync.dma_start(word_table[:].bitcast(I32), x_words[0].rearrange("p n t -> p (n t)").bitcast(I32))
+        ca_l = load_list(ca, "ca_l")
+        gain = sb.tile([P, PACK], F32, name="gain")
+        nc.sync.dma_start(gain[:], gs.rearrange("(p t) o -> p (t o)", t=PACK))
+        n2_l = load_list(n2, "n2_l")
+        n1_l = load_list(n1, "n1_l")
+        n4_l = load_list(n4, "n4_l")
+        n3_l = load_list(n3, "n3_l")
+
+        def gather_scales(lst, name):
+            dst = sb.tile([P, S], U8, name=name, align_bytes=64)
+            nc.vector.tensor_copy(dst[:], scale_table[:].indirect(lst[:]))
+            return dst
+
+        def deal_scales(src, name):
+            dst = sb.tile([P, S], U8, name=name, align_bytes=64)
+            nc.vector.tensor_copy(
+                dst[:].bitcast(I32).rearrange("p (t g w) -> p t g w", t=PACK, w=RUN // 4),
+                src[:].bitcast(I32).rearrange("p (g t w) -> p t g w", t=PACK, w=RUN // 4),
+            )
+            return dst
+
+        def gather_dealt_words(lst, name, tag):
+            dst = sb.tile([P, S], U32, name=name, tag=tag, align_bytes=64)
+            nc.vector.tensor_copy(
+                dst[:].rearrange("p (t g v) -> p g t v", t=PACK, v=RUN), word_table[:].indirect(lst[:])
+            )
+            return dst
+
+        xq_scales = gather_scales(offs_l, "xq_scales")
+        cb_picked = gather_scales(cb_l, "cb_picked")
+
+        w_bf = sb.tile([P, H * PACK], BF16, name="w_bf", align_bytes=64)
+        w_view = w_bf[:].rearrange("p (t m j) -> p m t j", t=PACK, j=PACK)
+        for h in range(2):
+            nc.scalar.copy(
+                w_view[:, h * (P // 2) : (h + 1) * (P // 2)],
+                w_raw[h][:].rearrange("p j (m t) -> p m t j", t=PACK),
+            )
+        w_codes = sb.tile([P, H], U32, name="w_codes", align_bytes=64)
+        w_scales = sb.tile([P, H], U8, name="w_scales", align_bytes=64)
+        nc.vector.quantize_mx(out=w_codes[:].bitcast(FP8X4), scales=w_scales[:], in_=w_bf[:])
+        cb_scales = deal_scales(cb_picked, "cb_scales")
+
+        xq_words = sb.tile([P, S], U32, name="xq_words", align_bytes=64)
+        nc.vector.tensor_copy(xq_words[:], word_table[:].indirect(offs_l[:]))
+        cb_words = gather_dealt_words(cb_l, "cb_words", "cb_words")
+        ca_picked = gather_scales(ca_l, "ca_picked")
+        ca_scales = deal_scales(ca_picked, "ca_scales")
+
+        def mx(dst, words, scales, t, rhs, rhs_scale):
+            cols = slice(t * P, (t + 1) * P)
+            nc.tensor.matmul_mx(
+                out=dst,
+                lhsT=words[:, cols].bitcast(FP8X4),
+                lhsT_scale=scales[:, cols],
+                rhs=rhs.bitcast(FP8X4),
+                rhs_scale=rhs_scale,
+                start=True,
+                stop=True,
+            )
+
+        y_ps = [psum.tile([P, S], F32, name=f"y_ps{t}", tag=f"ya{t}") for t in range(PACK)]
+        ys = [sb.tile([P, S], F32, name=f"ys{t}") for t in range(PACK)]
+        y_sb = sb.tile([P, PACK, S], F32, name="y_sb")
+        for t in range(PACK):
+            mx(y_ps[t][:], w_codes, w_scales, t, xq_words[:], xq_scales[:])
+        for t in range(PACK):
+            nc.scalar.activation(ys[t][:], y_ps[t][:], ACT.Copy, scale=gain[:, t : t + 1])
+        for t in range(PACK):
+            nc.scalar.copy(y_sb[:, t, :], y_ps[t][:])
+
+        second = [[sb.tile([P, HALF], F32, name=f"second{h}{t}") for t in range(PACK)] for h in range(2)]
+        diff = [sb.tile([P, PACK, HALF], F32, name=f"diff{h}", tag=f"diff{h}", align_bytes=64) for h in range(2)]
+        z_bf = [sb.tile([P, HALF, PACK], BF16, name=f"z_bf{h}", align_bytes=64) for h in range(2)]
+        z_codes = sb.tile([P, S], U32, name="z_codes", align_bytes=64)
+        z_scales = sb.tile([P, S], U8, name="z_scales", align_bytes=64)
+
+        def fetch_second(h, t):
+            nc.vector.tensor_copy(second[h][t][:], ys[t][:].indirect(half_list(n2_l, h)))
+
+        def fetch_diff(h, t):
+            nc.vector.tensor_tensor(
+                diff[h][:, t, :], ys[t][:].indirect(half_list(n1_l, h)), second[h][t][:], ALU.subtract
+            )
+
+        def make_z(h):
+            nc.vector.tensor_tensor(
+                z_bf[h][:].rearrange("p (c i) t -> p c t i", i=2),
+                diff[h][:].rearrange("p t (c i) -> p c t i", i=2),
+                y_sb[:, :, half_cols(h)].rearrange("p t (c i) -> p c t i", i=2),
+                ALU.mult,
+            )
+
+        def quantise_z(h):
+            nc.vector.quantize_mx(
+                out=z_codes[:, half_cols(h)].bitcast(FP8X4),
+                scales=z_scales[:, half_cols(h)],
+                in_=z_bf[h][:].rearrange("p c t -> p (c t)"),
+            )
+
+        b_ps = [psum.tile([P, S], F32, name=f"b_ps{t}") for t in range(PACK)]
+        b_win = [sb.tile([P, S], F32, name=f"b_win{t}") for t in range(PACK)]
+        b_own = [sb.tile([P, S], F32, name=f"b_own{t}") for t in range(PACK)]
+
+        def make_b(h):
+            for t in range(PACK):
+                mx(b_ps[t][:, half_cols(h)], cb_words, cb_scales, t, z_codes[:, half_cols(h)], z_scales[:, half_cols(h)])
+            for t in range(PACK):
+                for dst in (b_win, b_own):
+                    nc.scalar.activation(dst[t][:, half_cols(h)], b_ps[t][:, half_cols(h)], ACT.Abs, scale=0.0625)
+
+        fetch_second(0, 0)
+        for t in range(1, PACK):
+            fetch_second(0, t)
+            fetch_diff(0, t - 1)
+        fetch_second(1, 0)
+        fetch_diff(0, PACK - 1)
+        fetch_second(1, 1)
+        make_z(0)
+        fetch_diff(1, 0)
+        quantise_z(0)
+        make_b(0)
+        for t in range(2, PACK):
+            fetch_second(1, t)
+            fetch_diff(1, t - 1)
+        fetch_diff(1, PACK - 1)
+        make_z(1)
+        quantise_z(1)
+        make_b(1)
+        ca_words = gather_dealt_words(ca_l, "ca_words", "diff1")
+
+        a_ps = [psum.tile([P, S], F32, name=f"a_ps{t}", tag=f"ya{t}") for t in range(PACK)]
+        a_win = [sb.tile([P, S], F32, name=f"a_win{t}") for t in range(PACK)]
+        a_own = [sb.tile([P, S], F32, name=f"a_own{t}") for t in range(PACK)]
+        den = [sb.tile([P, S], F32, name=f"den{t}") for t in range(PACK)]
+        root = [sb.tile([P, S], F32, name=f"root{t}") for t in range(PACK)]
+        inv = [sb.tile([P, S], F32, name=f"inv{t}") for t in range(PACK)]
+        num = [sb.tile([P, S], F32, name=f"num{t}") for t in range(PACK)]
+        res = [sb.tile([P, S], F32, name=f"res{t}") for t in range(PACK)]
+        out_rows = out.rearrange("(g t v) j -> t g v j", t=PACK, v=RUN)
+
+        for t in range(PACK):
+            mx(a_ps[t][:], ca_words, ca_scales, t, z_codes[:], z_scales[:])
+
+        def make_a(t):
+            for dst in (a_win, a_own):
+                nc.scalar.activation(dst[t][:], a_ps[t][:], ACT.Copy, scale=-0.0625)
+
+        def make_den(t):
+            for h in range(2):
+                nc.vector.tensor_tensor(
+                    den[t][:, half_cols(h)], b_win[t][:].indirect(half_list(n4_l, h)), b_own[t][:, half_cols(h)], ALU.add
+                )
+
+        def make_inv(t):
+            nc.scalar.activation(root[t][:], den[t][:], ACT.Abs_reciprocal_sqrt, bias=half_const[:])
+            nc.scalar.activation(inv[t][:], root[t][:], ACT.Square)
+
+        def make_num(t, h):
+            nc.vector.tensor_tensor(
+                num[t][:, half_cols(h)], a_win[t][:].indirect(half_list(n3_l, h)), a_own[t][:, half_cols(h)], ALU.subtract
+            )
+
+        def finish(t, cols):
+            nc.vector.tensor_tensor(res[t][:, cols], num[t][:, cols], inv[t][:, cols], ALU.mult)
+            nc.sync.dma_start(out_rows[t][:, :, cols], res[t][:, cols])
+
+        whole = slice(0, S)
+        make_den(0)
+        make_a(0)
+        make_den(1)
+        make_inv(0)
+        make_num(0, 0)
+        make_num(0, 1)
+        make_a(1)
+        make_den(2)
+        make_inv(1)
+        finish(0, whole)
+        make_num(1, 0)
+        make_num(1, 1)
+        make_a(2)
+        make_den(3)
+        make_inv(2)
+        finish(1, whole)
+        make_a(3)
+        make_inv(3)
+        make_num(2, 0)
+        make_num(2, 1)
+        make_num(3, 0)
+        finish(2, whole)
+        make_num(3, 1)
+        finish(3, half_cols(0))
+        finish(3, half_cols(1))

@@ -49,13 +49,14 @@ def tile_picked_ccmpnormbwind_none_p_kernel(
         warm = sb.tile([P, 1], F32, name="warm")
         nc.scalar.activation(warm[:], half_const[:], ACT.Abs_reciprocal_sqrt)
 
+        offs_l = load_list(offs, "offs_l")
+        cb_l = load_list(cb, "cb_l")
+        ca_l = load_list(ca, "ca_l")
         for q in range(4):
             nc.sync.dma_start(
                 scale_table[32 * q : 32 * q + 4, :].bitcast(I32),
                 x_scales[0, 4 * q : 4 * q + 4, :].bitcast(I32),
             )
-        offs_l = load_list(offs, "offs_l")
-        cb_l = load_list(cb, "cb_l")
         w_raw = []
         for h in range(2):
             w_half = sb.tile([P, PACK, H // 2], F32, name=f"w_raw{h}")
@@ -65,7 +66,6 @@ def tile_picked_ccmpnormbwind_none_p_kernel(
             w_raw.append(w_half)
         word_table = sb.tile([P, T], U32, name="word_table", align_bytes=64)
         nc.sync.dma_start(word_table[:].bitcast(I32), x_words[0].rearrange("p n t -> p (n t)").bitcast(I32))
-        ca_l = load_list(ca, "ca_l")
         gain = sb.tile([P, PACK], F32, name="gain")
         nc.sync.dma_start(gain[:], gs.rearrange("(p t) o -> p (t o)", t=PACK))
         n2_l = load_list(n2, "n2_l")
@@ -95,6 +95,7 @@ def tile_picked_ccmpnormbwind_none_p_kernel(
 
         xq_scales = gather_scales(offs_l, "xq_scales")
         cb_picked = gather_scales(cb_l, "cb_picked")
+        ca_picked = gather_scales(ca_l, "ca_picked")
 
         w_bf = sb.tile([P, H * PACK], BF16, name="w_bf", align_bytes=64)
         w_view = w_bf[:].rearrange("p (t m j) -> p m t j", t=PACK, j=PACK)
@@ -111,7 +112,6 @@ def tile_picked_ccmpnormbwind_none_p_kernel(
         xq_words = sb.tile([P, S], U32, name="xq_words", align_bytes=64)
         nc.vector.tensor_copy(xq_words[:], word_table[:].indirect(offs_l[:]))
         cb_words = gather_dealt_words(cb_l, "cb_words", "cb_words")
-        ca_picked = gather_scales(ca_l, "ca_picked")
         ca_scales = deal_scales(ca_picked, "ca_scales")
 
         def mx(dst, words, scales, t, rhs, rhs_scale):
@@ -132,22 +132,22 @@ def tile_picked_ccmpnormbwind_none_p_kernel(
         for t in range(PACK):
             mx(y_ps[t][:], w_codes, w_scales, t, xq_words[:], xq_scales[:])
         for t in range(PACK):
-            nc.scalar.activation(ys[t][:], y_ps[t][:], ACT.Copy, scale=gain[:, t : t + 1])
+            nc.scalar.activation(ys[t][:, :S], y_ps[t][:], ACT.Copy, scale=gain[:, t : t + 1])
         for t in range(PACK):
             nc.scalar.copy(y_sb[:, t, :], y_ps[t][:])
 
-        second = [[sb.tile([P, HALF], F32, name=f"second{h}{t}") for t in range(PACK)] for h in range(2)]
-        diff = [sb.tile([P, PACK, HALF], F32, name=f"diff{h}", tag=f"diff{h}", align_bytes=64) for h in range(2)]
+        second = [sb.tile([P, S], F32, name=f"second{t}") for t in range(PACK)]
+        diff = [sb.tile([P, PACK, HALF], F32, name=f"diff{h}", tag="diff", align_bytes=64) for h in range(2)]
         z_bf = [sb.tile([P, HALF, PACK], BF16, name=f"z_bf{h}", align_bytes=64) for h in range(2)]
         z_codes = sb.tile([P, S], U32, name="z_codes", align_bytes=64)
         z_scales = sb.tile([P, S], U8, name="z_scales", align_bytes=64)
 
         def fetch_second(h, t):
-            nc.vector.tensor_copy(second[h][t][:], ys[t][:].indirect(half_list(n2_l, h)))
+            nc.vector.tensor_copy(second[t][:, half_cols(h)], ys[t][:].indirect(half_list(n2_l, h)))
 
         def fetch_diff(h, t):
             nc.vector.tensor_tensor(
-                diff[h][:, t, :], ys[t][:].indirect(half_list(n1_l, h)), second[h][t][:], ALU.subtract
+                diff[h][:, t, :], ys[t][:].indirect(half_list(n1_l, h)), second[t][:, half_cols(h)], ALU.subtract
             )
 
         def make_z(h):
@@ -166,7 +166,7 @@ def tile_picked_ccmpnormbwind_none_p_kernel(
             )
 
         b_ps = [psum.tile([P, S], F32, name=f"b_ps{t}") for t in range(PACK)]
-        b_win = [sb.tile([P, S], F32, name=f"b_win{t}") for t in range(PACK)]
+        b_win = [sb.tile([P, 2 * S], F32, name=f"b_win{t}") for t in range(PACK)]
         b_own = [sb.tile([P, S], F32, name=f"b_own{t}") for t in range(PACK)]
 
         def make_b(h):
@@ -176,28 +176,22 @@ def tile_picked_ccmpnormbwind_none_p_kernel(
                 for dst in (b_win, b_own):
                     nc.scalar.activation(dst[t][:, half_cols(h)], b_ps[t][:, half_cols(h)], ACT.Abs, scale=0.0625)
 
-        fetch_second(0, 0)
-        for t in range(1, PACK):
+        for t in range(PACK):
             fetch_second(0, t)
-            fetch_diff(0, t - 1)
-        fetch_second(1, 0)
-        fetch_diff(0, PACK - 1)
-        fetch_second(1, 1)
+            fetch_second(1, t)
+            fetch_diff(0, t)
         make_z(0)
-        fetch_diff(1, 0)
         quantise_z(0)
         make_b(0)
-        for t in range(2, PACK):
-            fetch_second(1, t)
-            fetch_diff(1, t - 1)
-        fetch_diff(1, PACK - 1)
+        for t in range(PACK):
+            fetch_diff(1, t)
         make_z(1)
         quantise_z(1)
         make_b(1)
-        ca_words = gather_dealt_words(ca_l, "ca_words", "diff1")
+        ca_words = gather_dealt_words(ca_l, "ca_words", "diff")
 
         a_ps = [psum.tile([P, S], F32, name=f"a_ps{t}", tag=f"ya{t}") for t in range(PACK)]
-        a_win = [sb.tile([P, S], F32, name=f"a_win{t}") for t in range(PACK)]
+        a_win = [sb.tile([P, 2 * S], F32, name=f"a_win{t}") for t in range(PACK)]
         a_own = [sb.tile([P, S], F32, name=f"a_own{t}") for t in range(PACK)]
         den = [sb.tile([P, S], F32, name=f"den{t}") for t in range(PACK)]
         root = [sb.tile([P, S], F32, name=f"root{t}") for t in range(PACK)]
@@ -206,18 +200,19 @@ def tile_picked_ccmpnormbwind_none_p_kernel(
         res = [sb.tile([P, S], F32, name=f"res{t}") for t in range(PACK)]
         out_rows = out.rearrange("(g t v) j -> t g v j", t=PACK, v=RUN)
 
-        for t in range(PACK):
+        a_order = (1, 0, 2, 3)
+        for t in a_order:
             mx(a_ps[t][:], ca_words, ca_scales, t, z_codes[:], z_scales[:])
 
         def make_a(t):
-            for dst in (a_win, a_own):
-                nc.scalar.activation(dst[t][:], a_ps[t][:], ACT.Copy, scale=-0.0625)
+            nc.scalar.activation(a_win[t][:, :S], a_ps[t][:], ACT.Copy, scale=-0.0625)
+            if t == 0:
+                nc.scalar.activation(a_own[t][:], a_ps[t][:], ACT.Copy, scale=-0.0625)
+            else:
+                nc.sync.dma_start(a_own[t][:], a_win[t][:, :S])
 
         def make_den(t):
-            for h in range(2):
-                nc.vector.tensor_tensor(
-                    den[t][:, half_cols(h)], b_win[t][:].indirect(half_list(n4_l, h)), b_own[t][:, half_cols(h)], ALU.add
-                )
+            nc.vector.tensor_tensor(den[t][:], b_win[t][:].indirect(n4_l[:]), b_own[t][:], ALU.add)
 
         def make_inv(t):
             nc.scalar.activation(root[t][:], den[t][:], ACT.Abs_reciprocal_sqrt, bias=half_const[:])
@@ -228,33 +223,23 @@ def tile_picked_ccmpnormbwind_none_p_kernel(
                 num[t][:, half_cols(h)], a_win[t][:].indirect(half_list(n3_l, h)), a_own[t][:, half_cols(h)], ALU.subtract
             )
 
+        def make_num_whole(t):
+            nc.vector.tensor_tensor(num[t][:], a_win[t][:].indirect(n3_l[:]), a_own[t][:], ALU.subtract)
+
         def finish(t, cols):
             nc.vector.tensor_tensor(res[t][:, cols], num[t][:, cols], inv[t][:, cols], ALU.mult)
             nc.sync.dma_start(out_rows[t][:, :, cols], res[t][:, cols])
 
         whole = slice(0, S)
-        make_den(0)
-        make_a(0)
-        make_den(1)
-        make_inv(0)
-        make_num(0, 0)
-        make_num(0, 1)
-        make_a(1)
-        make_den(2)
-        make_inv(1)
-        finish(0, whole)
-        make_num(1, 0)
-        make_num(1, 1)
-        make_a(2)
-        make_den(3)
-        make_inv(2)
-        finish(1, whole)
-        make_a(3)
-        make_inv(3)
-        make_num(2, 0)
-        make_num(2, 1)
-        make_num(3, 0)
-        finish(2, whole)
-        make_num(3, 1)
+        for t in range(PACK):
+            make_den(t)
+        for t in a_order:
+            make_a(t)
+        for t in range(PACK):
+            make_inv(t)
+        make_num_whole(0)
+        for t in range(1, PACK):
+            make_num_whole(t)
+            finish(t - 1, whole)
         finish(3, half_cols(0))
         finish(3, half_cols(1))

@@ -17,9 +17,14 @@ ACT = mybir.ActivationFunctionType
 
 P = 128
 PACK = 4
-HALF = S // 2
-LIST_COLS = S // 16
+TILES = 4
+LAST = TILES - 1
+STRIPE = 16
 RUN = 8
+HALF = S // 2
+QUARTER = S // 4
+WIDE = 2 * S
+SIXTEENTH = 0.0625
 
 
 def tile_picked_ccmpnormbwind_none_p_kernel(
@@ -31,23 +36,23 @@ def tile_picked_ccmpnormbwind_none_p_kernel(
         sb = ctx.enter_context(tc.tile_pool(name="sb", bufs=1))
         psum = ctx.enter_context(tc.psum_pool(name="psum", bufs=1))
 
+        whole = slice(0, S)
+        halves = [slice(h * HALF, (h + 1) * HALF) for h in range(2)]
+
+        def entries(lst, cols):
+            return lst[:, cols.start // STRIPE : cols.stop // STRIPE]
+
         def load_list(src, name):
-            dst = lists.tile([P, LIST_COLS], U16, name=name)
+            dst = lists.tile([P, S // STRIPE], U16, name=name)
             nc.sync.dma_start(dst[:], src)
             return dst
 
-        def half_cols(h):
-            return slice(h * HALF, (h + 1) * HALF)
-
-        def half_list(lst, h):
-            return lst[:, h * (LIST_COLS // 2) : (h + 1) * (LIST_COLS // 2)]
-
         scale_table = sb.tile([P, T], U8, name="scale_table", align_bytes=64)
         nc.vector.memset(scale_table[:].bitcast(I32), 0)
-        half_const = sb.tile([P, 1], F32, name="half_const")
-        nc.vector.memset(half_const[:], 0.5)
-        warm = sb.tile([P, 1], F32, name="warm")
-        nc.scalar.activation(warm[:], half_const[:], ACT.Abs_reciprocal_sqrt)
+        four = sb.tile([P, 1], F32, name="four")
+        nc.vector.memset(four[:], 4.0)
+        one_half = sb.tile([P, 1], F32, name="one_half")
+        nc.scalar.activation(one_half[:], four[:], ACT.Abs_reciprocal_sqrt)
 
         offs_l = load_list(offs, "offs_l")
         cb_l = load_list(cb, "cb_l")
@@ -57,17 +62,13 @@ def tile_picked_ccmpnormbwind_none_p_kernel(
                 scale_table[32 * q : 32 * q + 4, :].bitcast(I32),
                 x_scales[0, 4 * q : 4 * q + 4, :].bitcast(I32),
             )
-        w_raw = []
+        w_raw = [sb.tile([P, PACK, HALF], F32, name=f"w_raw{h}") for h in range(2)]
         for h in range(2):
-            w_half = sb.tile([P, PACK, H // 2], F32, name=f"w_raw{h}")
-            nc.sync.dma_start(
-                w_half[:], w1[:, h * (H // 2) : (h + 1) * (H // 2)].rearrange("(p j) c -> p j c", j=PACK)
-            )
-            w_raw.append(w_half)
+            nc.sync.dma_start(w_raw[h][:], w1[:, halves[h]].rearrange("(p j) c -> p j c", j=PACK))
         word_table = sb.tile([P, T], U32, name="word_table", align_bytes=64)
         nc.sync.dma_start(word_table[:].bitcast(I32), x_words[0].rearrange("p n t -> p (n t)").bitcast(I32))
-        gain = sb.tile([P, PACK], F32, name="gain")
-        nc.sync.dma_start(gain[:], gs.rearrange("(p t) o -> p (t o)", t=PACK))
+        gain = sb.tile([P, TILES], F32, name="gain")
+        nc.sync.dma_start(gain[:], gs.rearrange("(p t) o -> p (t o)", t=TILES))
         n2_l = load_list(n2, "n2_l")
         n1_l = load_list(n1, "n1_l")
         n4_l = load_list(n4, "n4_l")
@@ -81,15 +82,15 @@ def tile_picked_ccmpnormbwind_none_p_kernel(
         def deal_scales(src, name):
             dst = sb.tile([P, S], U8, name=name, align_bytes=64)
             nc.vector.tensor_copy(
-                dst[:].bitcast(I32).rearrange("p (t g w) -> p t g w", t=PACK, w=RUN // 4),
-                src[:].bitcast(I32).rearrange("p (g t w) -> p t g w", t=PACK, w=RUN // 4),
+                dst[:].bitcast(I32).rearrange("p (t g w) -> p t g w", t=TILES, w=RUN // 4),
+                src[:].bitcast(I32).rearrange("p (g t w) -> p t g w", t=TILES, w=RUN // 4),
             )
             return dst
 
         def gather_dealt_words(lst, name, tag):
             dst = sb.tile([P, S], U32, name=name, tag=tag, align_bytes=64)
             nc.vector.tensor_copy(
-                dst[:].rearrange("p (t g v) -> p g t v", t=PACK, v=RUN), word_table[:].indirect(lst[:])
+                dst[:].rearrange("p (t g v) -> p g t v", t=TILES, v=RUN), word_table[:].indirect(lst[:])
             )
             return dst
 
@@ -98,11 +99,11 @@ def tile_picked_ccmpnormbwind_none_p_kernel(
         ca_picked = gather_scales(ca_l, "ca_picked")
 
         w_bf = sb.tile([P, H * PACK], BF16, name="w_bf", align_bytes=64)
-        w_view = w_bf[:].rearrange("p (t m j) -> p m t j", t=PACK, j=PACK)
+        w_view = w_bf[:].rearrange("p (t m j) -> p m t j", t=TILES, j=PACK)
         for h in range(2):
             nc.scalar.copy(
                 w_view[:, h * (P // 2) : (h + 1) * (P // 2)],
-                w_raw[h][:].rearrange("p j (m t) -> p m t j", t=PACK),
+                w_raw[h][:].rearrange("p j (m t) -> p m t j", t=TILES),
             )
         w_codes = sb.tile([P, H], U32, name="w_codes", align_bytes=64)
         w_scales = sb.tile([P, H], U8, name="w_scales", align_bytes=64)
@@ -110,7 +111,8 @@ def tile_picked_ccmpnormbwind_none_p_kernel(
         cb_scales = deal_scales(cb_picked, "cb_scales")
 
         xq_words = sb.tile([P, S], U32, name="xq_words", align_bytes=64)
-        nc.vector.tensor_copy(xq_words[:], word_table[:].indirect(offs_l[:]))
+        for cols in halves:
+            nc.vector.tensor_copy(xq_words[:, cols], word_table[:].indirect(entries(offs_l, cols)))
         cb_words = gather_dealt_words(cb_l, "cb_words", "cb_words")
         ca_scales = deal_scales(ca_picked, "ca_scales")
 
@@ -126,120 +128,142 @@ def tile_picked_ccmpnormbwind_none_p_kernel(
                 stop=True,
             )
 
-        y_ps = [psum.tile([P, S], F32, name=f"y_ps{t}", tag=f"ya{t}") for t in range(PACK)]
-        ys = [sb.tile([P, S], F32, name=f"ys{t}") for t in range(PACK)]
-        y_sb = sb.tile([P, PACK, S], F32, name="y_sb")
-        for t in range(PACK):
-            mx(y_ps[t][:], w_codes, w_scales, t, xq_words[:], xq_scales[:])
-        for t in range(PACK):
-            nc.scalar.activation(ys[t][:, :S], y_ps[t][:], ACT.Copy, scale=gain[:, t : t + 1])
-        for t in range(PACK):
-            nc.scalar.copy(y_sb[:, t, :], y_ps[t][:])
+        y_ps = [psum.tile([P, S], F32, name=f"y_ps{t}", tag=f"ya{t}") for t in range(TILES)]
+        y_late = psum.tile([P, HALF], F32, name="y_late", tag=f"b{LAST}")
+        y_parts = [(0, halves[0], y_ps[0][:, :HALF]), (0, halves[1], y_late[:])]
+        y_parts.extend((t, whole, y_ps[t][:]) for t in range(1, TILES))
+        y_gained = [sb.tile([P, S], F32, name=f"y_gained{t}") for t in range(TILES)]
+        y_plain = sb.tile([P, TILES, S], F32, name="y_plain")
+        for t, cols, bank in y_parts:
+            mx(bank, w_codes, w_scales, t, xq_words[:, cols], xq_scales[:, cols])
+        for t, cols, bank in y_parts:
+            nc.scalar.activation(y_gained[t][:, cols], bank, ACT.Copy, scale=gain[:, t : t + 1])
+        for t, cols, bank in y_parts:
+            nc.scalar.copy(y_plain[:, t, cols], bank)
 
-        second = [sb.tile([P, S], F32, name=f"second{t}") for t in range(PACK)]
-        diff = [sb.tile([P, PACK, HALF], F32, name=f"diff{h}", tag="diff", align_bytes=64) for h in range(2)]
+        second = [sb.tile([P, S], F32, name=f"second{t}") for t in range(TILES)]
+        diff = [sb.tile([P, TILES, HALF], F32, name=f"diff{h}", tag="diff", align_bytes=64) for h in range(2)]
         z_bf = [sb.tile([P, HALF, PACK], BF16, name=f"z_bf{h}", align_bytes=64) for h in range(2)]
         z_codes = sb.tile([P, S], U32, name="z_codes", align_bytes=64)
         z_scales = sb.tile([P, S], U8, name="z_scales", align_bytes=64)
 
-        def fetch_second(h, t):
-            nc.vector.tensor_copy(second[t][:, half_cols(h)], ys[t][:].indirect(half_list(n2_l, h)))
+        def within(h, cols):
+            return slice(cols.start - h * HALF, cols.stop - h * HALF)
 
-        def fetch_diff(h, t):
+        def fetch_second(t, cols):
+            nc.vector.tensor_copy(second[t][:, cols], y_gained[t][:].indirect(entries(n2_l, cols)))
+
+        def fetch_diff(h, t, cols):
             nc.vector.tensor_tensor(
-                diff[h][:, t, :], ys[t][:].indirect(half_list(n1_l, h)), second[t][:, half_cols(h)], ALU.subtract
+                diff[h][:, t, within(h, cols)],
+                y_gained[t][:].indirect(entries(n1_l, cols)),
+                second[t][:, cols],
+                ALU.subtract,
             )
 
-        def make_z(h):
+        def make_z(h, cols):
             nc.vector.tensor_tensor(
-                z_bf[h][:].rearrange("p (c i) t -> p c t i", i=2),
-                diff[h][:].rearrange("p t (c i) -> p c t i", i=2),
-                y_sb[:, :, half_cols(h)].rearrange("p t (c i) -> p c t i", i=2),
+                z_bf[h][:, within(h, cols)].rearrange("p (c i) t -> p c t i", i=2),
+                diff[h][:, :, within(h, cols)].rearrange("p t (c i) -> p c t i", i=2),
+                y_plain[:, :, cols].rearrange("p t (c i) -> p c t i", i=2),
                 ALU.mult,
             )
 
-        def quantise_z(h):
+        def quantise_z(h, cols):
             nc.vector.quantize_mx(
-                out=z_codes[:, half_cols(h)].bitcast(FP8X4),
-                scales=z_scales[:, half_cols(h)],
-                in_=z_bf[h][:].rearrange("p c t -> p (c t)"),
+                out=z_codes[:, cols].bitcast(FP8X4),
+                scales=z_scales[:, cols],
+                in_=z_bf[h][:, within(h, cols)].rearrange("p c t -> p (c t)"),
             )
 
-        b_ps = [psum.tile([P, S], F32, name=f"b_ps{t}") for t in range(PACK)]
-        b_win = [sb.tile([P, 2 * S], F32, name=f"b_win{t}") for t in range(PACK)]
-        b_own = [sb.tile([P, S], F32, name=f"b_own{t}") for t in range(PACK)]
+        def close_half(h):
+            quarters = [slice(h * HALF + i * QUARTER, h * HALF + (i + 1) * QUARTER) for i in range(2)]
+            for cols in quarters:
+                fetch_diff(h, LAST, cols)
+            for cols in quarters:
+                make_z(h, cols)
+            for cols in quarters:
+                quantise_z(h, cols)
 
-        def make_b(h):
-            for t in range(PACK):
-                mx(b_ps[t][:, half_cols(h)], cb_words, cb_scales, t, z_codes[:, half_cols(h)], z_scales[:, half_cols(h)])
-            for t in range(PACK):
+        b_ps = [psum.tile([P, S], F32, name=f"b_ps{t}", tag=f"b{t}") for t in range(TILES)]
+        b_win = [sb.tile([P, WIDE], F32, name=f"b_win{t}") for t in range(TILES)]
+        b_own = [sb.tile([P, S], F32, name=f"b_own{t}") for t in range(TILES)]
+
+        def make_abs_b(cols):
+            for t in range(TILES):
+                mx(b_ps[t][:, cols], cb_words, cb_scales, t, z_codes[:, cols], z_scales[:, cols])
+            for t in range(TILES):
                 for dst in (b_win, b_own):
-                    nc.scalar.activation(dst[t][:, half_cols(h)], b_ps[t][:, half_cols(h)], ACT.Abs, scale=0.0625)
+                    nc.scalar.activation(dst[t][:, cols], b_ps[t][:, cols], ACT.Abs, scale=SIXTEENTH)
 
-        for t in range(PACK):
-            fetch_second(0, t)
-            fetch_second(1, t)
-            fetch_diff(0, t)
-        make_z(0)
-        quantise_z(0)
-        make_b(0)
-        for t in range(PACK):
-            fetch_diff(1, t)
-        make_z(1)
-        quantise_z(1)
-        make_b(1)
+        for t in range(TILES):
+            for cols in halves:
+                fetch_second(t, cols)
+            if t < LAST:
+                fetch_diff(0, t, halves[0])
+        close_half(0)
+        make_abs_b(halves[0])
+        for t in range(LAST):
+            fetch_diff(1, t, halves[1])
+        close_half(1)
+        make_abs_b(halves[1])
         ca_words = gather_dealt_words(ca_l, "ca_words", "diff")
 
-        a_ps = [psum.tile([P, S], F32, name=f"a_ps{t}", tag=f"ya{t}") for t in range(PACK)]
-        a_win = [sb.tile([P, 2 * S], F32, name=f"a_win{t}") for t in range(PACK)]
-        a_own = [sb.tile([P, S], F32, name=f"a_own{t}") for t in range(PACK)]
-        den = [sb.tile([P, S], F32, name=f"den{t}") for t in range(PACK)]
-        root = [sb.tile([P, S], F32, name=f"root{t}") for t in range(PACK)]
-        inv = [sb.tile([P, S], F32, name=f"inv{t}") for t in range(PACK)]
-        num = [sb.tile([P, S], F32, name=f"num{t}") for t in range(PACK)]
-        res = [sb.tile([P, S], F32, name=f"res{t}") for t in range(PACK)]
-        out_rows = out.rearrange("(g t v) j -> t g v j", t=PACK, v=RUN)
+        a_ps = [psum.tile([P, S], F32, name=f"a_ps{t}", tag=f"ya{t}") for t in range(TILES)]
+        a_win = [sb.tile([P, WIDE], F32, name=f"a_win{t}") for t in range(TILES)]
+        a_own = [sb.tile([P, S], F32, name=f"a_own{t}") for t in range(TILES)]
+        den = [sb.tile([P, S], F32, name=f"den{t}") for t in range(TILES)]
+        root = [sb.tile([P, S], F32, name=f"root{t}") for t in range(TILES)]
+        inv = [sb.tile([P, S], F32, name=f"inv{t}") for t in range(TILES)]
+        num = [sb.tile([P, S], F32, name=f"num{t}") for t in range(TILES)]
+        res = [sb.tile([P, S], F32, name=f"res{t}") for t in range(TILES)]
+        out_rows = out.rearrange("(g t v) j -> t g v j", t=TILES, v=RUN)
 
-        a_order = (1, 0, 2, 3)
-        for t in a_order:
+        by_dma = tuple(range(1, LAST))
+        for t in by_dma + (0, LAST):
             mx(a_ps[t][:], ca_words, ca_scales, t, z_codes[:], z_scales[:])
 
-        def make_a(t):
-            nc.scalar.activation(a_win[t][:, :S], a_ps[t][:], ACT.Copy, scale=-0.0625)
-            if t == 0:
-                nc.scalar.activation(a_own[t][:], a_ps[t][:], ACT.Copy, scale=-0.0625)
-            else:
+        def copy_minus_a(t):
+            nc.scalar.activation(a_win[t][:, :S], a_ps[t][:], ACT.Copy, scale=-SIXTEENTH)
+            if t in by_dma:
                 nc.sync.dma_start(a_own[t][:], a_win[t][:, :S])
+            else:
+                nc.scalar.activation(a_own[t][:], a_ps[t][:], ACT.Copy, scale=-SIXTEENTH)
 
-        def make_den(t):
-            nc.vector.tensor_tensor(den[t][:], b_win[t][:].indirect(n4_l[:]), b_own[t][:], ALU.add)
-
-        def make_inv(t):
-            nc.scalar.activation(root[t][:], den[t][:], ACT.Abs_reciprocal_sqrt, bias=half_const[:])
-            nc.scalar.activation(inv[t][:], root[t][:], ACT.Square)
-
-        def make_num(t, h):
+        def make_den(t, cols):
             nc.vector.tensor_tensor(
-                num[t][:, half_cols(h)], a_win[t][:].indirect(half_list(n3_l, h)), a_own[t][:, half_cols(h)], ALU.subtract
+                den[t][:, cols], b_win[t][:].indirect(entries(n4_l, cols)), b_own[t][:, cols], ALU.add
             )
 
-        def make_num_whole(t):
-            nc.vector.tensor_tensor(num[t][:], a_win[t][:].indirect(n3_l[:]), a_own[t][:], ALU.subtract)
+        def make_inv(t):
+            nc.scalar.activation(root[t][:], den[t][:], ACT.Abs_reciprocal_sqrt, bias=one_half[:])
+            nc.scalar.activation(inv[t][:], root[t][:], ACT.Square)
+
+        def make_num(t, cols):
+            nc.vector.tensor_tensor(
+                num[t][:, cols], a_win[t][:].indirect(entries(n3_l, cols)), a_own[t][:, cols], ALU.subtract
+            )
 
         def finish(t, cols):
             nc.vector.tensor_tensor(res[t][:, cols], num[t][:, cols], inv[t][:, cols], ALU.mult)
             nc.sync.dma_start(out_rows[t][:, :, cols], res[t][:, cols])
 
-        whole = slice(0, S)
-        for t in range(PACK):
-            make_den(t)
-        for t in a_order:
-            make_a(t)
-        for t in range(PACK):
+        for cols in halves:
+            make_den(0, cols)
+        for t in range(1, TILES):
+            make_den(t, whole)
+        for t in by_dma + (0,):
+            copy_minus_a(t)
+        for t in range(LAST):
             make_inv(t)
-        make_num_whole(0)
-        for t in range(1, PACK):
-            make_num_whole(t)
+        copy_minus_a(LAST)
+        make_inv(LAST)
+        make_num(0, whole)
+        for t in range(1, LAST):
+            make_num(t, whole)
             finish(t - 1, whole)
-        finish(3, half_cols(0))
-        finish(3, half_cols(1))
+        finish(LAST - 1, whole)
+        for cols in halves:
+            make_num(LAST, cols)
+        for cols in halves:
+            finish(LAST, cols)

from contextlib import ExitStack

import concourse.mybir as mybir

K, T, S, H, C = 512, 2048, 512, 512, 512
FLOPS = 2 * K * H * S + 2 * 2 * H * C * S

F32 = mybir.dt.float32
BF16 = mybir.dt.bfloat16
I32 = mybir.dt.int32
U32 = mybir.dt.uint32
U16 = mybir.dt.uint16
U8 = mybir.dt.uint8
FP8X4 = mybir.dt.float8_e4m3fn_x4
ALU = mybir.AluOpType
ACT = mybir.ActivationFunctionType

P = 128
PACK = 4
TILES = 4
LAST = TILES - 1
STRIPE = 16
RUN = 8
HALF = S // 2
QUARTER = S // 4
WIDE = 2 * S
SIXTEENTH = 0.0625


def tile_picked_ccmpnormbwind_none_p_kernel(
    tc, x_words, x_scales, w1, gs, offs, n1, n2, ca, cb, n3, n4, out
):
    nc = tc.nc
    with ExitStack() as ctx:
        lists = ctx.enter_context(tc.tile_pool(name="lists", bufs=1))
        sb = ctx.enter_context(tc.tile_pool(name="sb", bufs=1))
        psum = ctx.enter_context(tc.psum_pool(name="psum", bufs=1))

        whole = slice(0, S)
        halves = [slice(h * HALF, (h + 1) * HALF) for h in range(2)]

        def entries(lst, cols):
            return lst[:, cols.start // STRIPE : cols.stop // STRIPE]

        def load_list(src, name):
            dst = lists.tile([P, S // STRIPE], U16, name=name)
            nc.sync.dma_start(dst[:], src)
            return dst

        scale_table = sb.tile([P, T], U8, name="scale_table", align_bytes=64)
        nc.vector.memset(scale_table[:].bitcast(I32), 0)
        four = sb.tile([P, 1], F32, name="four")
        nc.vector.memset(four[:], 4.0)
        one_half = sb.tile([P, 1], F32, name="one_half")
        nc.scalar.activation(one_half[:], four[:], ACT.Abs_reciprocal_sqrt)

        offs_l = load_list(offs, "offs_l")
        cb_l = load_list(cb, "cb_l")
        ca_l = load_list(ca, "ca_l")
        for q in range(4):
            nc.sync.dma_start(
                scale_table[32 * q : 32 * q + 4, :].bitcast(I32),
                x_scales[0, 4 * q : 4 * q + 4, :].bitcast(I32),
            )
        w_raw = [sb.tile([P, PACK, HALF], F32, name=f"w_raw{h}") for h in range(2)]
        for h in range(2):
            nc.sync.dma_start(w_raw[h][:], w1[:, halves[h]].rearrange("(p j) c -> p j c", j=PACK))
        word_table = sb.tile([P, T], U32, name="word_table", align_bytes=64)
        nc.sync.dma_start(word_table[:].bitcast(I32), x_words[0].rearrange("p n t -> p (n t)").bitcast(I32))
        gain = sb.tile([P, TILES], F32, name="gain")
        nc.sync.dma_start(gain[:], gs.rearrange("(p t) o -> p (t o)", t=TILES))
        n2_l = load_list(n2, "n2_l")
        n1_l = load_list(n1, "n1_l")
        n4_l = load_list(n4, "n4_l")
        n3_l = load_list(n3, "n3_l")

        def gather_scales(lst, name):
            dst = sb.tile([P, S], U8, name=name, align_bytes=64)
            nc.vector.tensor_copy(dst[:], scale_table[:].indirect(lst[:]))
            return dst

        def deal_scales(src, name):
            dst = sb.tile([P, S], U8, name=name, align_bytes=64)
            nc.vector.tensor_copy(
                dst[:].bitcast(I32).rearrange("p (t g w) -> p t g w", t=TILES, w=RUN // 4),
                src[:].bitcast(I32).rearrange("p (g t w) -> p t g w", t=TILES, w=RUN // 4),
            )
            return dst

        def gather_dealt_words(lst, name, tag):
            dst = sb.tile([P, S], U32, name=name, tag=tag, align_bytes=64)
            nc.vector.tensor_copy(
                dst[:].rearrange("p (t g v) -> p g t v", t=TILES, v=RUN), word_table[:].indirect(lst[:])
            )
            return dst

        xq_scales = gather_scales(offs_l, "xq_scales")
        cb_picked = gather_scales(cb_l, "cb_picked")
        ca_picked = gather_scales(ca_l, "ca_picked")

        w_bf = sb.tile([P, H * PACK], BF16, name="w_bf", align_bytes=64)
        w_view = w_bf[:].rearrange("p (t m j) -> p m t j", t=TILES, j=PACK)
        for h in range(2):
            nc.scalar.copy(
                w_view[:, h * (P // 2) : (h + 1) * (P // 2)],
                w_raw[h][:].rearrange("p j (m t) -> p m t j", t=TILES),
            )
        w_codes = sb.tile([P, H], U32, name="w_codes", align_bytes=64)
        w_scales = sb.tile([P, H], U8, name="w_scales", align_bytes=64)
        nc.vector.quantize_mx(out=w_codes[:].bitcast(FP8X4), scales=w_scales[:], in_=w_bf[:])
        cb_scales = deal_scales(cb_picked, "cb_scales")

        xq_words = sb.tile([P, S], U32, name="xq_words", align_bytes=64)
        for cols in halves:
            nc.vector.tensor_copy(xq_words[:, cols], word_table[:].indirect(entries(offs_l, cols)))
        cb_words = gather_dealt_words(cb_l, "cb_words", "cb_words")
        ca_scales = deal_scales(ca_picked, "ca_scales")

        def mx(dst, words, scales, t, rhs, rhs_scale):
            cols = slice(t * P, (t + 1) * P)
            nc.tensor.matmul_mx(
                out=dst,
                lhsT=words[:, cols].bitcast(FP8X4),
                lhsT_scale=scales[:, cols],
                rhs=rhs.bitcast(FP8X4),
                rhs_scale=rhs_scale,
                start=True,
                stop=True,
            )

        y_ps = [psum.tile([P, S], F32, name=f"y_ps{t}", tag=f"ya{t}") for t in range(TILES)]
        y_late = psum.tile([P, HALF], F32, name="y_late", tag=f"b{LAST}")
        y_parts = [(0, halves[0], y_ps[0][:, :HALF]), (0, halves[1], y_late[:])]
        y_parts.extend((t, whole, y_ps[t][:]) for t in range(1, TILES))
        y_gained = [sb.tile([P, S], F32, name=f"y_gained{t}") for t in range(TILES)]
        y_plain = sb.tile([P, TILES, S], F32, name="y_plain")
        for t, cols, bank in y_parts:
            mx(bank, w_codes, w_scales, t, xq_words[:, cols], xq_scales[:, cols])
        for t, cols, bank in y_parts:
            nc.scalar.activation(y_gained[t][:, cols], bank, ACT.Copy, scale=gain[:, t : t + 1])
        for t, cols, bank in y_parts:
            nc.scalar.copy(y_plain[:, t, cols], bank)

        second = [sb.tile([P, S], F32, name=f"second{t}") for t in range(TILES)]
        diff = [sb.tile([P, TILES, HALF], F32, name=f"diff{h}", tag="diff", align_bytes=64) for h in range(2)]
        z_bf = [sb.tile([P, HALF, PACK], BF16, name=f"z_bf{h}", align_bytes=64) for h in range(2)]
        z_codes = sb.tile([P, S], U32, name="z_codes", align_bytes=64)
        z_scales = sb.tile([P, S], U8, name="z_scales", align_bytes=64)

        def within(h, cols):
            return slice(cols.start - h * HALF, cols.stop - h * HALF)

        def fetch_second(t, cols):
            nc.vector.tensor_copy(second[t][:, cols], y_gained[t][:].indirect(entries(n2_l, cols)))

        def fetch_diff(h, t, cols):
            nc.vector.tensor_tensor(
                diff[h][:, t, within(h, cols)],
                y_gained[t][:].indirect(entries(n1_l, cols)),
                second[t][:, cols],
                ALU.subtract,
            )

        def make_z(h, cols):
            nc.vector.tensor_tensor(
                z_bf[h][:, within(h, cols)].rearrange("p (c i) t -> p c t i", i=2),
                diff[h][:, :, within(h, cols)].rearrange("p t (c i) -> p c t i", i=2),
                y_plain[:, :, cols].rearrange("p t (c i) -> p c t i", i=2),
                ALU.mult,
            )

        def quantise_z(h, cols):
            nc.vector.quantize_mx(
                out=z_codes[:, cols].bitcast(FP8X4),
                scales=z_scales[:, cols],
                in_=z_bf[h][:, within(h, cols)].rearrange("p c t -> p (c t)"),
            )

        def close_half(h):
            quarters = [slice(h * HALF + i * QUARTER, h * HALF + (i + 1) * QUARTER) for i in range(2)]
            for cols in quarters:
                fetch_diff(h, LAST, cols)
            for cols in quarters:
                make_z(h, cols)
            for cols in quarters:
                quantise_z(h, cols)

        b_ps = [psum.tile([P, S], F32, name=f"b_ps{t}", tag=f"b{t}") for t in range(TILES)]
        b_win = [sb.tile([P, WIDE], F32, name=f"b_win{t}") for t in range(TILES)]
        b_own = [sb.tile([P, S], F32, name=f"b_own{t}") for t in range(TILES)]

        def make_abs_b(cols):
            for t in range(TILES):
                mx(b_ps[t][:, cols], cb_words, cb_scales, t, z_codes[:, cols], z_scales[:, cols])
            for t in range(TILES):
                for dst in (b_win, b_own):
                    nc.scalar.activation(dst[t][:, cols], b_ps[t][:, cols], ACT.Abs, scale=SIXTEENTH)

        for t in range(TILES):
            for cols in halves:
                fetch_second(t, cols)
            if t < LAST:
                fetch_diff(0, t, halves[0])
        close_half(0)
        make_abs_b(halves[0])
        for t in range(LAST):
            fetch_diff(1, t, halves[1])
        close_half(1)
        make_abs_b(halves[1])
        ca_words = gather_dealt_words(ca_l, "ca_words", "diff")

        a_ps = [psum.tile([P, S], F32, name=f"a_ps{t}", tag=f"ya{t}") for t in range(TILES)]
        a_win = [sb.tile([P, WIDE], F32, name=f"a_win{t}") for t in range(TILES)]
        a_own = [sb.tile([P, S], F32, name=f"a_own{t}") for t in range(TILES)]
        den = [sb.tile([P, S], F32, name=f"den{t}") for t in range(TILES)]
        root = [sb.tile([P, S], F32, name=f"root{t}") for t in range(TILES)]
        inv = [sb.tile([P, S], F32, name=f"inv{t}") for t in range(TILES)]
        num = [sb.tile([P, S], F32, name=f"num{t}") for t in range(TILES)]
        res = [sb.tile([P, S], F32, name=f"res{t}") for t in range(TILES)]
        out_rows = out.rearrange("(g t v) j -> t g v j", t=TILES, v=RUN)

        by_dma = tuple(range(1, LAST))
        for t in by_dma + (0, LAST):
            mx(a_ps[t][:], ca_words, ca_scales, t, z_codes[:], z_scales[:])

        def copy_minus_a(t):
            nc.scalar.activation(a_win[t][:, :S], a_ps[t][:], ACT.Copy, scale=-SIXTEENTH)
            if t in by_dma:
                nc.sync.dma_start(a_own[t][:], a_win[t][:, :S])
            else:
                nc.scalar.activation(a_own[t][:], a_ps[t][:], ACT.Copy, scale=-SIXTEENTH)

        def make_den(t, cols):
            nc.vector.tensor_tensor(
                den[t][:, cols], b_win[t][:].indirect(entries(n4_l, cols)), b_own[t][:, cols], ALU.add
            )

        def make_inv(t):
            nc.scalar.activation(root[t][:], den[t][:], ACT.Abs_reciprocal_sqrt, bias=one_half[:])
            nc.scalar.activation(inv[t][:], root[t][:], ACT.Square)

        def make_num(t, cols):
            nc.vector.tensor_tensor(
                num[t][:, cols], a_win[t][:].indirect(entries(n3_l, cols)), a_own[t][:, cols], ALU.subtract
            )

        def finish(t, cols):
            nc.vector.tensor_tensor(res[t][:, cols], num[t][:, cols], inv[t][:, cols], ALU.mult)
            nc.sync.dma_start(out_rows[t][:, :, cols], res[t][:, cols])

        for cols in halves:
            make_den(0, cols)
        for t in range(1, TILES):
            make_den(t, whole)
        for t in by_dma + (0,):
            copy_minus_a(t)
        for t in range(LAST):
            make_inv(t)
        copy_minus_a(LAST)
        make_inv(LAST)
        make_num(0, whole)
        for t in range(1, LAST):
            make_num(t, whole)
            finish(t - 1, whole)
        finish(LAST - 1, whole)
        for cols in halves:
            make_num(LAST, cols)
        for cols in halves:
            finish(LAST, cols)
